import numpy as np
import ml_dtypes


def mxq(x, axis, fmt="e4m3"):
    dtype, down = {"e4m3": (ml_dtypes.float8_e4m3fn, 7), "e5m2": (ml_dtypes.float8_e5m2, 14)}[fmt]
    v = np.moveaxis(np.asarray(x, np.float32).astype(ml_dtypes.bfloat16).astype(np.float64), axis, -1)
    blocks = v.reshape(v.shape[:-1] + (-1, 32))
    amax = np.abs(blocks).max(-1, keepdims=True)
    byte = np.maximum(np.where(amax > 0, np.frexp(amax)[1] - 1 + 127, 0) - down, 1)
    scale = np.exp2(byte - 127.0)
    codes = (blocks / scale).astype(np.float32).astype(dtype).astype(np.float64)
    return np.moveaxis((codes * scale).reshape(v.shape), -1, axis)


WIDE = False


def mx_kscale(k):
    if not WIDE:
        return np.ones(k)
    levels = np.array([10, -10, 5, -5, 0])
    if k % 512:
        return np.exp2(np.random.permutation(np.resize(levels, k // 32))).repeat(32)
    a = np.empty((k // 512, 16))
    for p in range(k // 512):
        a[p, :8] = np.random.permutation(np.resize(levels, 8))
        for g in range(8):
            far = levels[np.abs(levels - a[p, g]) >= 10]
            a[p, g + 8] = far[np.random.randint(len(far))]
    return np.exp2(a.ravel()).repeat(32)


def f64(x):
    return np.asarray(x).astype(np.float64)


def striped(idx):
    return np.tile(idx.reshape(-1, 16).T, (8, 1)).astype(np.uint16)


def unstriped(offs):
    return offs[:16].T.reshape(-1).astype(np.int64)


def striped8(idx):
    return np.concatenate([x.reshape(-1, 16).T for x in idx]).astype(np.uint16)


def runs(offs, k):
    lists = np.stack([offs[16 * r : 16 * r + 16].T.reshape(-1) for r in range(8)]).astype(np.int64)
    return lists[np.arange(k) % 512 // 64]


def pack_weight(w):
    k, n = w.shape
    w = f64(np.asarray(w, np.float32).astype(ml_dtypes.bfloat16)).reshape(k // 32, 32, n)
    amax = np.abs(w).max(1)
    byte = np.clip(np.where(amax > 0, np.frexp(amax)[1] - 1 + 127 - 7, 1), 1, 254)
    scaled = (w * np.exp2(127.0 - byte)[:, None, :]).reshape(k, n).astype(np.float32)
    words = np.ascontiguousarray(scaled.reshape(k // 512, 128, 4, n).transpose(0, 1, 3, 2)).astype(ml_dtypes.float8_e4m3fn).view(np.uint8)
    return words, np.ascontiguousarray(byte.astype(np.uint8).reshape(k // 512, 16, n))


def unpack_weight(words, scales):
    g, p, n, _ = words.shape
    vals = np.ascontiguousarray(words).view(ml_dtypes.float8_e4m3fn).astype(np.float64) * np.repeat(np.exp2(scales.astype(np.float64) - 127.0), 8, axis=1)[..., None]
    return vals.transpose(0, 1, 3, 2).reshape(g * 512, n)


K, T, S, G, H, W, C = 512, 1024, 256, 2048, 512, 192, 512


def setup_inputs():
    n = np.random.standard_normal
    s = mx_kscale(K)[:, None]
    packed_xT = pack_weight(n((K, T)) * s)
    packed_dT = pack_weight(n((K, G)) / s)
    return {
        "x_words": packed_xT[0],
        "x_scales": packed_xT[1],
        "d_words": packed_dT[0],
        "d_scales": packed_dT[1],
        "gs": (np.random.uniform(0.5, 1.5, (K, 1)) / s).astype(np.float32),
        "offs": striped(np.random.permutation(T)[:S]),
        "k1": striped8(np.random.randint(0, G, (8, H))),
        "n1": striped(np.random.permutation(S)[:W]),
        "n2": striped(np.random.permutation(S)[:W]),
        "cand": striped(np.random.permutation(T)[:C]),
        "two": striped(np.random.permutation(T)[:S]),
        "k2": striped8(np.random.randint(0, G, (8, H))),
        "n3": striped(np.random.permutation(S)),
        "n4": striped(np.random.permutation(S)),
    }


def reference(x_words, x_scales, d_words, d_scales, gs, offs, k1, n1, n2, cand, two, k2, n3, n4):
    x_cand = unpack_weight(x_words, x_scales)[:, unstriped(cand)]
    d_k1 = unpack_weight(d_words, d_scales)[np.arange(K)[:, None], runs(k1, K)]
    xq = unpack_weight(x_words, x_scales)[:, unstriped(offs)]
    h = 0.0625 * (d_k1.T @ xq)
    pa = h[:, unstriped(n2)]
    old = h[:, unstriped(n1)]
    ra = np.minimum(pa, old) - (0.5 * pa)
    ds = h.copy()
    ds[:, unstriped(n1)] = ra
    z = f64(gs) * ds
    a = 0.0625 * ((x_cand.T @ mxq(z, 0, "e4m3")))
    d_k2 = unpack_weight(d_words, d_scales)[np.arange(K)[:, None], runs(k2, K)]
    x_two = unpack_weight(x_words, x_scales)[:, unstriped(two)]
    b = 0.0625 * (d_k2.T @ x_two)
    return 0.75 * (a * b[:, unstriped(n4)] - (a[:, unstriped(n3)] * b))

@@ -1,0 +1,181 @@
+from contextlib import ExitStack
+
+import concourse.mybir as mybir
+
+F32 = mybir.dt.float32
+BF16 = mybir.dt.bfloat16
+I32 = mybir.dt.int32
+U32 = mybir.dt.uint32
+U16 = mybir.dt.uint16
+U8 = mybir.dt.uint8
+FP8X4 = mybir.dt.float8_e4m3fn_x4
+ALU = mybir.AluOpType
+COPY = mybir.ActivationFunctionType.Copy
+
+P = 128
+K, T, S, G, H, W, C = 512, 1024, 256, 2048, 512, 192, 512
+PACK = 4
+TILES = 4
+SPARE = 8
+FLOPS = 3 * 2 * K * H * S
+
+
+def tile_picked_pqcjcrossbkmin_none_p_kernel(
+    tc, x_words, x_scales, d_words, d_scales, gs, offs, k1, n1, n2, cand, two, k2, n3, n4, out
+):
+    nc = tc.nc
+    with ExitStack() as ctx:
+        keep = ctx.enter_context(tc.tile_pool(name="keep", bufs=1))
+        psum = ctx.enter_context(tc.psum_pool(name="psum", bufs=1))
+
+        def sb(name, width, dtype):
+            return keep.tile([P, width], dtype, name=name, align_bytes=64)
+
+        def load_list(name, src, entries):
+            tile = sb(name, entries // 16, U16)
+            nc.sync.dma_start(tile[:], src)
+            return tile
+
+        def gather(name, window, offsets, entries, dtype):
+            tile = sb(name, entries, dtype)
+            nc.vector.tensor_copy(tile[:], window[:].indirect(offsets[:]))
+            return tile
+
+        def fetch(name, window, offsets, entries):
+            tile = sb(name, entries, F32)
+            nc.scalar.activation(tile[:], window[:].indirect(offsets[:]), COPY)
+            return tile
+
+        def product(bank, lhs_words, lhs_scales, t, rhs_words, rhs_scales):
+            cols = slice(P * t, P * (t + 1))
+            nc.tensor.matmul_mx(
+                out=bank[:, 0:S],
+                lhsT=lhs_words[:, cols].bitcast(FP8X4),
+                lhsT_scale=lhs_scales[:, cols],
+                rhs=rhs_words[:].bitcast(FP8X4),
+                rhs_scale=rhs_scales[:],
+                start=True,
+                stop=True,
+            )
+
+        ds_win = sb("ds_win", G, U8)
+        xs_win = sb("xs_win", T, U8)
+        nc.vector.memset(ds_win[:].bitcast(I32), 0)
+        nc.gpsimd.memset(xs_win[:].bitcast(I32), 0)
+
+        k1_t = load_list("k1_t", k1, H)
+        offs_t = load_list("offs_t", offs, S)
+        k2_t = load_list("k2_t", k2, H)
+        two_t = load_list("two_t", two, S)
+        nc.sync.dma_start(ds_win[0:P:8, :].bitcast(I32), d_scales[0].bitcast(I32))
+        dw_win = sb("dw_win", G, U32)
+        nc.sync.dma_start(dw_win[:].bitcast(I32), d_words[0].rearrange("p n t -> p (n t)").bitcast(I32))
+        xw_win = sb("xw_win", T, U32)
+        nc.sync.dma_start(xw_win[:].bitcast(I32), x_words[0].rearrange("p n t -> p (n t)").bitcast(I32))
+        for q in range(4):
+            nc.gpsimd.dma_start(xs_win[32 * q : 32 * q + 4, :].bitcast(I32), x_scales[0, 4 * q : 4 * q + 4, :].bitcast(I32))
+        gs_t = sb("gs_t", PACK, F32)
+        nc.gpsimd.dma_start(gs_t[:], gs.rearrange("(p t) o -> p (t o)", t=PACK))
+        n2_t = load_list("n2_t", n2, W)
+        n1_t = load_list("n1_t", n1, W)
+        cand_t = load_list("cand_t", cand, C)
+        n4_t = load_list("n4_t", n4, S)
+        n3_t = load_list("n3_t", n3, S)
+
+        k2_scales = sb("k2_scales", H, U8)
+        nc.gpsimd.memset(k2_scales[:].bitcast(I32), 0)
+        a_win = [sb("a_win%d" % t, S + SPARE, F32) for t in range(TILES)]
+        b_win = [sb("b_win%d" % t, S + SPARE, F32) for t in range(TILES)]
+        for win in b_win + a_win:
+            nc.gpsimd.memset(win[:, S : S + SPARE], 0.0)
+
+        k1_raw_scales = gather("k1_raw_scales", ds_win, k1_t, H, U8)
+        k1_scales = sb("k1_scales", H, U8)
+        nc.vector.tensor_copy(
+            k1_scales[:].rearrange("p (t c i) -> p c t i", t=PACK, i=16),
+            k1_raw_scales[:].rearrange("p (c i t) -> p c t i", t=PACK, i=16),
+        )
+        for r in range(1, 4):
+            nc.scalar.dma_start(k1_scales[r:P:32, :].bitcast(I32), k1_scales[8 * r : P : 32, :].bitcast(I32))
+        offs_scales = gather("offs_scales", xs_win, offs_t, S, U8)
+        k1_raw_words = gather("k1_raw_words", dw_win, k1_t, H, U32)
+        offs_words = gather("offs_words", xw_win, offs_t, S, U32)
+        k1_words = sb("k1_words", H, U32)
+        nc.vector.tensor_copy(
+            k1_words[:].rearrange("p (t c i) -> p c t i", t=PACK, i=4),
+            k1_raw_words[:].rearrange("p (c i t) -> p c t i", t=PACK, i=4),
+        )
+        banks = [psum.tile([P, 512], F32, name="bank%d" % i) for i in range(8)]
+        h_win = [sb("h_win%d" % t, S, F32) for t in range(TILES)]
+        for t in range(TILES):
+            product(banks[t], k1_words, k1_scales, t, offs_words, offs_scales)
+
+        k2_raw_scales = gather("k2_raw_scales", ds_win, k2_t, H, U8)
+        for r in range(4):
+            nc.sync.dma_start(k2_scales[r:P:32, :].bitcast(I32), k2_raw_scales[8 * r : P : 32, :].bitcast(I32))
+
+        z = sb("z", S * PACK, BF16)
+        z_slots = z[:].rearrange("p (j t) -> p j t", t=PACK)
+        later = [
+            ("k2_words", dw_win, k2_t, H, U32),
+            ("two_words", xw_win, two_t, S, U32),
+            ("two_scales", xs_win, two_t, S, U8),
+            ("cand_words", xw_win, cand_t, C, U32),
+            ("cand_scales", xs_win, cand_t, C, U8),
+        ]
+        got = {}
+        ra = {}
+
+        def front(t):
+            nc.scalar.activation(h_win[t][:], banks[t][:, 0:S], COPY, scale=0.0625)
+            pa = fetch("pa%d" % t, h_win[t], n2_t, W)
+            old = fetch("old%d" % t, h_win[t], n1_t, W)
+            low = sb("low%d" % t, W, F32)
+            nc.vector.tensor_tensor(low[:], pa[:], old[:], ALU.min)
+            ra[t] = sb("ra%d" % t, W, F32)
+            nc.vector.scalar_tensor_tensor(ra[t][:], pa[:], -0.5, low[:], ALU.mult, ALU.add)
+
+        def back(t):
+            nc.scalar.activation(h_win[t][:].indirect(n1_t[:]), ra[t][:], COPY)
+            nc.vector.tensor_scalar(z_slots[:, :, t], h_win[t][:], gs_t[:, t : t + 1], None, ALU.mult)
+
+        def more(i):
+            got[later[i][0]] = gather(*later[i])
+
+        front(0)
+        more(0)
+        front(1)
+        more(1)
+        more(2)
+        back(0)
+        for t in range(TILES):
+            product(banks[TILES + t], got["k2_words"], k2_scales, t, got["two_words"], got["two_scales"])
+        front(2)
+        more(3)
+        back(1)
+        front(3)
+        more(4)
+        back(2)
+        for t in range(TILES):
+            nc.vector.tensor_scalar(b_win[t][:, 0:S], banks[TILES + t][:, 0:S], 0.75 * 0.0625 * 0.0625, None, ALU.mult)
+        back(3)
+
+        z_words = sb("z_words", S, U32)
+        z_scales = sb("z_scales", S, U8)
+        nc.vector.quantize_mx(out=z_words[:].bitcast(FP8X4), scales=z_scales[:], in_=z[:])
+        b4 = [fetch("b4_%d" % t, b_win[t], n4_t, S) for t in range(TILES)]
+        for t in range(TILES):
+            product(banks[t], got["cand_words"], got["cand_scales"], t, z_words, z_scales)
+        first = {}
+        for t in range(TILES):
+            nc.vector.tensor_copy(a_win[t][:, 0:S], banks[t][:, 0:S])
+        for t in range(TILES):
+            first[t] = sb("first%d" % t, S, F32)
+            nc.vector.tensor_tensor(first[t][:], a_win[t][:, 0:S], b4[t][:], ALU.mult)
+        for t in range(TILES):
+            a3 = fetch("a3_%d" % t, a_win[t], n3_t, S)
+            second = sb("second%d" % t, S, F32)
+            nc.vector.tensor_tensor(second[:], a3[:], b_win[t][:, 0:S], ALU.mult)
+            res = sb("res%d" % t, S, F32)
+            nc.vector.tensor_tensor(res[:], first[t][:], second[:], ALU.subtract)
+            nc.sync.dma_start(out[P * t : P * (t + 1), :], res[:])

@@ -28,16 +28,16 @@ def tile_picked_pqcjcrossbkmin_none_p_kernel(
         keep = ctx.enter_context(tc.tile_pool(name="keep", bufs=1))
         psum = ctx.enter_context(tc.psum_pool(name="psum", bufs=1))
 
-        def sb(name, width, dtype):
-            return keep.tile([P, width], dtype, name=name, align_bytes=64)
+        def sb(name, width, dtype, tag=None):
+            return keep.tile([P, width], dtype, name=name, tag=tag or name, align_bytes=64)
 
         def load_list(name, src, entries):
             tile = sb(name, entries // 16, U16)
             nc.sync.dma_start(tile[:], src)
             return tile
 
-        def gather(name, window, offsets, entries, dtype):
-            tile = sb(name, entries, dtype)
+        def gather(name, window, offsets, entries, dtype, tag=None):
+            tile = sb(name, entries, dtype, tag)
             nc.vector.tensor_copy(tile[:], window[:].indirect(offsets[:]))
             return tile
 
@@ -60,22 +60,23 @@ def tile_picked_pqcjcrossbkmin_none_p_kernel(
 
         ds_win = sb("ds_win", G, U8)
         xs_win = sb("xs_win", T, U8)
-        nc.vector.memset(ds_win[:].bitcast(I32), 0)
+        nc.gpsimd.memset(ds_win[:].bitcast(I32), 0)
         nc.gpsimd.memset(xs_win[:].bitcast(I32), 0)
 
         k1_t = load_list("k1_t", k1, H)
-        offs_t = load_list("offs_t", offs, S)
-        k2_t = load_list("k2_t", k2, H)
-        two_t = load_list("two_t", two, S)
         nc.sync.dma_start(ds_win[0:P:8, :].bitcast(I32), d_scales[0].bitcast(I32))
+        offs_t = load_list("offs_t", offs, S)
         dw_win = sb("dw_win", G, U32)
         nc.sync.dma_start(dw_win[:].bitcast(I32), d_words[0].rearrange("p n t -> p (n t)").bitcast(I32))
         xw_win = sb("xw_win", T, U32)
-        nc.sync.dma_start(xw_win[:].bitcast(I32), x_words[0].rearrange("p n t -> p (n t)").bitcast(I32))
         for q in range(4):
-            nc.gpsimd.dma_start(xs_win[32 * q : 32 * q + 4, :].bitcast(I32), x_scales[0, 4 * q : 4 * q + 4, :].bitcast(I32))
+            if q == 3:
+                nc.sync.dma_start(xw_win[:].bitcast(I32), x_words[0].rearrange("p n t -> p (n t)").bitcast(I32))
+            nc.sync.dma_start(xs_win[32 * q : 32 * q + 4, :].bitcast(I32), x_scales[0, 4 * q : 4 * q + 4, :].bitcast(I32))
         gs_t = sb("gs_t", PACK, F32)
         nc.gpsimd.dma_start(gs_t[:], gs.rearrange("(p t) o -> p (t o)", t=PACK))
+        k2_t = load_list("k2_t", k2, H)
+        two_t = load_list("two_t", two, S)
         n2_t = load_list("n2_t", n2, W)
         n1_t = load_list("n1_t", n1, W)
         cand_t = load_list("cand_t", cand, C)
@@ -85,8 +86,7 @@ def tile_picked_pqcjcrossbkmin_none_p_kernel(
         k2_scales = sb("k2_scales", H, U8)
         nc.gpsimd.memset(k2_scales[:].bitcast(I32), 0)
         a_win = [sb("a_win%d" % t, S + SPARE, F32) for t in range(TILES)]
-        b_win = [sb("b_win%d" % t, S + SPARE, F32) for t in range(TILES)]
-        for win in b_win + a_win:
+        for win in a_win:
             nc.gpsimd.memset(win[:, S : S + SPARE], 0.0)
 
         k1_raw_scales = gather("k1_raw_scales", ds_win, k1_t, H, U8)
@@ -97,7 +97,6 @@ def tile_picked_pqcjcrossbkmin_none_p_kernel(
         )
         for r in range(1, 4):
             nc.scalar.dma_start(k1_scales[r:P:32, :].bitcast(I32), k1_scales[8 * r : P : 32, :].bitcast(I32))
-        offs_scales = gather("offs_scales", xs_win, offs_t, S, U8)
         k1_raw_words = gather("k1_raw_words", dw_win, k1_t, H, U32)
         offs_words = gather("offs_words", xw_win, offs_t, S, U32)
         k1_words = sb("k1_words", H, U32)
@@ -105,6 +104,7 @@ def tile_picked_pqcjcrossbkmin_none_p_kernel(
             k1_words[:].rearrange("p (t c i) -> p c t i", t=PACK, i=4),
             k1_raw_words[:].rearrange("p (c i t) -> p c t i", t=PACK, i=4),
         )
+        offs_scales = gather("offs_scales", xs_win, offs_t, S, U8)
         banks = [psum.tile([P, 512], F32, name="bank%d" % i) for i in range(8)]
         h_win = [sb("h_win%d" % t, S, F32) for t in range(TILES)]
         for t in range(TILES):
@@ -113,69 +113,52 @@ def tile_picked_pqcjcrossbkmin_none_p_kernel(
         k2_raw_scales = gather("k2_raw_scales", ds_win, k2_t, H, U8)
         for r in range(4):
             nc.sync.dma_start(k2_scales[r:P:32, :].bitcast(I32), k2_raw_scales[8 * r : P : 32, :].bitcast(I32))
+        k2_words = gather("k2_words", dw_win, k2_t, H, U32)
+        two_words = gather("two_words", xw_win, two_t, S, U32)
+        two_scales = gather("two_scales", xs_win, two_t, S, U8)
+        for t in range(TILES):
+            product(banks[TILES + t], k2_words, k2_scales, t, two_words, two_scales)
 
         z = sb("z", S * PACK, BF16)
         z_slots = z[:].rearrange("p (j t) -> p j t", t=PACK)
-        later = [
-            ("k2_words", dw_win, k2_t, H, U32),
-            ("two_words", xw_win, two_t, S, U32),
-            ("two_scales", xs_win, two_t, S, U8),
-            ("cand_words", xw_win, cand_t, C, U32),
-            ("cand_scales", xs_win, cand_t, C, U8),
-        ]
-        got = {}
-        ra = {}
-
-        def front(t):
+        ra = []
+        for t in range(TILES):
             nc.scalar.activation(h_win[t][:], banks[t][:, 0:S], COPY, scale=0.0625)
             pa = fetch("pa%d" % t, h_win[t], n2_t, W)
             old = fetch("old%d" % t, h_win[t], n1_t, W)
             low = sb("low%d" % t, W, F32)
             nc.vector.tensor_tensor(low[:], pa[:], old[:], ALU.min)
-            ra[t] = sb("ra%d" % t, W, F32)
+            ra.append(sb("ra%d" % t, W, F32))
             nc.vector.scalar_tensor_tensor(ra[t][:], pa[:], -0.5, low[:], ALU.mult, ALU.add)
-
-        def back(t):
+        for t in range(TILES):
             nc.scalar.activation(h_win[t][:].indirect(n1_t[:]), ra[t][:], COPY)
-            nc.vector.tensor_scalar(z_slots[:, :, t], h_win[t][:], gs_t[:, t : t + 1], None, ALU.mult)
 
-        def more(i):
-            got[later[i][0]] = gather(*later[i])
-
-        front(0)
-        more(0)
-        front(1)
-        more(1)
-        more(2)
-        back(0)
+        cand_words = gather("cand_words", xw_win, cand_t, C, U32, "low2")
+        cand_scales = gather("cand_scales", xs_win, cand_t, C, U8, "low3")
+        b_win = [sb("b_win%d" % t, S + SPARE, F32, tag) for t, tag in enumerate(["pa3", "old3", "ra0", "ra1"])]
         for t in range(TILES):
-            product(banks[TILES + t], got["k2_words"], k2_scales, t, got["two_words"], got["two_scales"])
-        front(2)
-        more(3)
-        back(1)
-        front(3)
-        more(4)
-        back(2)
-        for t in range(TILES):
+            nc.gpsimd.memset(b_win[t][:, S : S + SPARE], 0.0)
             nc.vector.tensor_scalar(b_win[t][:, 0:S], banks[TILES + t][:, 0:S], 0.75 * 0.0625 * 0.0625, None, ALU.mult)
-        back(3)
+        for t in range(TILES):
+            nc.vector.tensor_scalar(z_slots[:, :, t], h_win[t][:], gs_t[:, t : t + 1], None, ALU.mult)
 
         z_words = sb("z_words", S, U32)
         z_scales = sb("z_scales", S, U8)
         nc.vector.quantize_mx(out=z_words[:].bitcast(FP8X4), scales=z_scales[:], in_=z[:])
         b4 = [fetch("b4_%d" % t, b_win[t], n4_t, S) for t in range(TILES)]
         for t in range(TILES):
-            product(banks[t], got["cand_words"], got["cand_scales"], t, z_words, z_scales)
-        first = {}
+            product(banks[t], cand_words, cand_scales, t, z_words, z_scales)
         for t in range(TILES):
             nc.vector.tensor_copy(a_win[t][:, 0:S], banks[t][:, 0:S])
         for t in range(TILES):
-            first[t] = sb("first%d" % t, S, F32)
-            nc.vector.tensor_tensor(first[t][:], a_win[t][:, 0:S], b4[t][:], ALU.mult)
-        for t in range(TILES):
+            first = sb("first%d" % t, S, F32)
+            nc.vector.tensor_tensor(first[:], banks[t][:, 0:S], b4[t][:], ALU.mult)
             a3 = fetch("a3_%d" % t, a_win[t], n3_t, S)
             second = sb("second%d" % t, S, F32)
-            nc.vector.tensor_tensor(second[:], a3[:], b_win[t][:, 0:S], ALU.mult)
+            nc.vector.scalar_tensor_tensor(
+                second[:], banks[TILES + t][:, 0:S], 0.75 * 0.0625 * 0.0625, a3[:], ALU.mult, ALU.mult
+            )
             res = sb("res%d" % t, S, F32)
-            nc.vector.tensor_tensor(res[:], first[t][:], second[:], ALU.subtract)
+            last = nc.vector if t == TILES - 1 else nc.gpsimd
+            last.tensor_tensor(res[:], first[:], second[:], ALU.subtract)
             nc.sync.dma_start(out[P * t : P * (t + 1), :], res[:])

@@ -66,22 +66,21 @@ def tile_picked_pqcjcrossbkmin_none_p_kernel(
         k1_t = load_list("k1_t", k1, H)
         nc.sync.dma_start(ds_win[0:P:8, :].bitcast(I32), d_scales[0].bitcast(I32))
         offs_t = load_list("offs_t", offs, S)
+        for q in range(4):
+            nc.sync.dma_start(xs_win[32 * q : 32 * q + 4, :].bitcast(I32), x_scales[0, 4 * q : 4 * q + 4, :].bitcast(I32))
         dw_win = sb("dw_win", G, U32)
         nc.sync.dma_start(dw_win[:].bitcast(I32), d_words[0].rearrange("p n t -> p (n t)").bitcast(I32))
-        xw_win = sb("xw_win", T, U32)
-        for q in range(4):
-            if q == 3:
-                nc.sync.dma_start(xw_win[:].bitcast(I32), x_words[0].rearrange("p n t -> p (n t)").bitcast(I32))
-            nc.sync.dma_start(xs_win[32 * q : 32 * q + 4, :].bitcast(I32), x_scales[0, 4 * q : 4 * q + 4, :].bitcast(I32))
-        gs_t = sb("gs_t", PACK, F32)
-        nc.gpsimd.dma_start(gs_t[:], gs.rearrange("(p t) o -> p (t o)", t=PACK))
-        k2_t = load_list("k2_t", k2, H)
-        two_t = load_list("two_t", two, S)
         n2_t = load_list("n2_t", n2, W)
         n1_t = load_list("n1_t", n1, W)
-        cand_t = load_list("cand_t", cand, C)
         n4_t = load_list("n4_t", n4, S)
+        xw_win = sb("xw_win", T, U32)
+        nc.sync.dma_start(xw_win[:].bitcast(I32), x_words[0].rearrange("p n t -> p (n t)").bitcast(I32))
+        k2_t = load_list("k2_t", k2, H)
+        two_t = load_list("two_t", two, S)
+        cand_t = load_list("cand_t", cand, C)
         n3_t = load_list("n3_t", n3, S)
+        gs_t = sb("gs_t", PACK, F32)
+        nc.gpsimd.dma_start(gs_t[:], gs.rearrange("(p t) o -> p (t o)", t=PACK))
 
         k2_scales = sb("k2_scales", H, U8)
         nc.gpsimd.memset(k2_scales[:].bitcast(I32), 0)
@@ -97,19 +96,21 @@ def tile_picked_pqcjcrossbkmin_none_p_kernel(
         )
         for r in range(1, 4):
             nc.scalar.dma_start(k1_scales[r:P:32, :].bitcast(I32), k1_scales[8 * r : P : 32, :].bitcast(I32))
+        offs_scales = gather("offs_scales", xs_win, offs_t, S, U8)
         k1_raw_words = gather("k1_raw_words", dw_win, k1_t, H, U32)
-        offs_words = gather("offs_words", xw_win, offs_t, S, U32)
         k1_words = sb("k1_words", H, U32)
         nc.vector.tensor_copy(
             k1_words[:].rearrange("p (t c i) -> p c t i", t=PACK, i=4),
             k1_raw_words[:].rearrange("p (c i t) -> p c t i", t=PACK, i=4),
         )
-        offs_scales = gather("offs_scales", xs_win, offs_t, S, U8)
+        offs_words = gather("offs_words", xw_win, offs_t, S, U32)
         banks = [psum.tile([P, 512], F32, name="bank%d" % i) for i in range(8)]
         h_win = [sb("h_win%d" % t, S, F32) for t in range(TILES)]
         for t in range(TILES):
             product(banks[t], k1_words, k1_scales, t, offs_words, offs_scales)
 
+        for t in range(2, TILES):
+            nc.vector.tensor_scalar(h_win[t][:], banks[t][:, 0:S], 0.0625, None, ALU.mult)
         k2_raw_scales = gather("k2_raw_scales", ds_win, k2_t, H, U8)
         for r in range(4):
             nc.sync.dma_start(k2_scales[r:P:32, :].bitcast(I32), k2_raw_scales[8 * r : P : 32, :].bitcast(I32))
@@ -123,7 +124,8 @@ def tile_picked_pqcjcrossbkmin_none_p_kernel(
         z_slots = z[:].rearrange("p (j t) -> p j t", t=PACK)
         ra = []
         for t in range(TILES):
-            nc.scalar.activation(h_win[t][:], banks[t][:, 0:S], COPY, scale=0.0625)
+            if t < 2:
+                nc.scalar.activation(h_win[t][:], banks[t][:, 0:S], COPY, scale=0.0625)
             pa = fetch("pa%d" % t, h_win[t], n2_t, W)
             old = fetch("old%d" % t, h_win[t], n1_t, W)
             low = sb("low%d" % t, W, F32)
@@ -135,30 +137,59 @@ def tile_picked_pqcjcrossbkmin_none_p_kernel(
 
         cand_words = gather("cand_words", xw_win, cand_t, C, U32, "low2")
         cand_scales = gather("cand_scales", xs_win, cand_t, C, U8, "low3")
-        b_win = [sb("b_win%d" % t, S + SPARE, F32, tag) for t, tag in enumerate(["pa3", "old3", "ra0", "ra1"])]
-        for t in range(TILES):
+        b_win = []
+
+        def empty_b(t, tag):
+            b_win.append(sb("b_win%d" % t, S + SPARE, F32, tag))
             nc.gpsimd.memset(b_win[t][:, S : S + SPARE], 0.0)
-            nc.vector.tensor_scalar(b_win[t][:, 0:S], banks[TILES + t][:, 0:S], 0.75 * 0.0625 * 0.0625, None, ALU.mult)
+            if t == 2:
+                nc.scalar.activation(b_win[t][:, 0:S], banks[TILES + t][:, 0:S], COPY, scale=0.75 * 0.0625 * 0.0625)
+            else:
+                nc.vector.tensor_scalar(b_win[t][:, 0:S], banks[TILES + t][:, 0:S], 0.75 * 0.0625 * 0.0625, None, ALU.mult)
+
+        empty_b(0, "pa3")
+        empty_b(1, "old3")
         for t in range(TILES):
             nc.vector.tensor_scalar(z_slots[:, :, t], h_win[t][:], gs_t[:, t : t + 1], None, ALU.mult)
 
         z_words = sb("z_words", S, U32)
         z_scales = sb("z_scales", S, U8)
         nc.vector.quantize_mx(out=z_words[:].bitcast(FP8X4), scales=z_scales[:], in_=z[:])
+        empty_b(2, "ra1")
+        empty_b(3, "h_win3")
         b4 = [fetch("b4_%d" % t, b_win[t], n4_t, S) for t in range(TILES)]
         for t in range(TILES):
             product(banks[t], cand_words, cand_scales, t, z_words, z_scales)
         for t in range(TILES):
             nc.vector.tensor_copy(a_win[t][:, 0:S], banks[t][:, 0:S])
+        OUT_SCALE = 0.75 * 0.0625 * 0.0625
+        first = []
         for t in range(TILES):
-            first = sb("first%d" % t, S, F32)
-            nc.vector.tensor_tensor(first[:], banks[t][:, 0:S], b4[t][:], ALU.mult)
-            a3 = fetch("a3_%d" % t, a_win[t], n3_t, S)
-            second = sb("second%d" % t, S, F32)
+            first.append(sb("first%d" % t, S, F32))
+            if t < 2:
+                nc.gpsimd.tensor_tensor(first[t][:], a_win[t][:, 0:S], b4[t][:], ALU.mult)
+            else:
+                nc.vector.tensor_tensor(first[t][:], banks[t][:, 0:S], b4[t][:], ALU.mult)
+        pieces = [(0, 0, S), (1, 0, S), (2, 0, S), (3, 0, S // 2), (3, S // 2, S)]
+        res = [sb("res%d" % t, S, F32) for t in range(TILES)]
+        second = {}
+
+        def make_second(t, lo, hi):
+            a3 = sb("a3_%d_%d" % (t, lo), hi - lo, F32)
+            nc.scalar.activation(a3[:], a_win[t][:].indirect(n3_t[:, lo // 16 : hi // 16]), COPY)
+            second[t, lo] = sb("second%d_%d" % (t, lo), hi - lo, F32)
             nc.vector.scalar_tensor_tensor(
-                second[:], banks[TILES + t][:, 0:S], 0.75 * 0.0625 * 0.0625, a3[:], ALU.mult, ALU.mult
+                second[t, lo][:], banks[TILES + t][:, lo:hi], OUT_SCALE, a3[:], ALU.mult, ALU.mult
             )
-            res = sb("res%d" % t, S, F32)
-            last = nc.vector if t == TILES - 1 else nc.gpsimd
-            last.tensor_tensor(res[:], first[:], second[:], ALU.subtract)
-            nc.sync.dma_start(out[P * t : P * (t + 1), :], res[:])
+
+        def finish(t, lo, hi):
+            engine = nc.gpsimd if t < 2 else nc.vector
+            engine.tensor_tensor(res[t][:, lo:hi], first[t][:, lo:hi], second[t, lo][:], ALU.subtract)
+            if hi == S:
+                nc.sync.dma_start(out[P * t : P * (t + 1), :], res[t][:])
+
+        make_second(*pieces[0])
+        for before, piece in zip(pieces, pieces[1:]):
+            make_second(*piece)
+            finish(*before)
+        finish(*pieces[-1])

@@ -13,10 +13,26 @@ ALU = mybir.AluOpType
 COPY = mybir.ActivationFunctionType.Copy
 
 P = 128
-K, T, S, G, H, W, C = 512, 1024, 256, 2048, 512, 192, 512
+K = 512
+T = 1024
+G = 2048
+S = 256
+H = 512
+C = 512
+W = 192
 PACK = 4
 TILES = 4
+QUADRANT = 32
+BLOCK_ROWS = 8
+LIST_ROWS = 16
+LINE_BYTES = 16
+BANK = 512
 SPARE = 8
+PAIR = 2
+H_ON_SCALAR = 2
+ON_GPSIMD = 2
+H_SCALE = 0.0625
+OUT_SCALE = 0.75 * 0.0625 * 0.0625
 FLOPS = 3 * 2 * K * H * S
 
 
@@ -28,22 +44,30 @@ def tile_picked_pqcjcrossbkmin_none_p_kernel(
         keep = ctx.enter_context(tc.tile_pool(name="keep", bufs=1))
         psum = ctx.enter_context(tc.psum_pool(name="psum", bufs=1))
 
-        def sb(name, width, dtype, tag=None):
-            return keep.tile([P, width], dtype, name=name, tag=tag or name, align_bytes=64)
+        def sb(name, width, dtype, reuse=None):
+            return keep.tile([P, width], dtype, name=name, tag=reuse or name, align_bytes=64)
 
         def load_list(name, src, entries):
-            tile = sb(name, entries // 16, U16)
+            tile = sb(name, entries // LIST_ROWS, U16)
             nc.sync.dma_start(tile[:], src)
             return tile
 
-        def gather(name, window, offsets, entries, dtype, tag=None):
-            tile = sb(name, entries, dtype, tag)
+        def load_words(name, src, columns):
+            tile = sb(name, columns, U32)
+            nc.sync.dma_start(tile[:].bitcast(I32), src[0].rearrange("p n t -> p (n t)").bitcast(I32))
+            return tile
+
+        def gather(name, window, offsets, entries, dtype, reuse=None):
+            tile = sb(name, entries, dtype, reuse)
             nc.vector.tensor_copy(tile[:], window[:].indirect(offsets[:]))
             return tile
 
-        def fetch(name, window, offsets, entries):
-            tile = sb(name, entries, F32)
-            nc.scalar.activation(tile[:], window[:].indirect(offsets[:]), COPY)
+        def deal(name, src, dtype, per_line):
+            tile = sb(name, H, dtype)
+            nc.vector.tensor_copy(
+                tile[:].rearrange("p (t c i) -> p c t i", t=PACK, i=per_line),
+                src[:].rearrange("p (c i t) -> p c t i", t=PACK, i=per_line),
+            )
             return tile
 
         def product(bank, lhs_words, lhs_scales, t, rhs_words, rhs_scales):
@@ -58,23 +82,24 @@ def tile_picked_pqcjcrossbkmin_none_p_kernel(
                 stop=True,
             )
 
-        ds_win = sb("ds_win", G, U8)
-        xs_win = sb("xs_win", T, U8)
-        nc.gpsimd.memset(ds_win[:].bitcast(I32), 0)
-        nc.gpsimd.memset(xs_win[:].bitcast(I32), 0)
+        d_scale_win = sb("ds_win", G, U8)
+        x_scale_win = sb("xs_win", T, U8)
+        nc.gpsimd.memset(d_scale_win[:].bitcast(I32), 0)
+        nc.gpsimd.memset(x_scale_win[:].bitcast(I32), 0)
 
         k1_t = load_list("k1_t", k1, H)
-        nc.sync.dma_start(ds_win[0:P:8, :].bitcast(I32), d_scales[0].bitcast(I32))
+        nc.sync.dma_start(d_scale_win[0:P:BLOCK_ROWS, :].bitcast(I32), d_scales[0].bitcast(I32))
         offs_t = load_list("offs_t", offs, S)
-        for q in range(4):
-            nc.sync.dma_start(xs_win[32 * q : 32 * q + 4, :].bitcast(I32), x_scales[0, 4 * q : 4 * q + 4, :].bitcast(I32))
-        dw_win = sb("dw_win", G, U32)
-        nc.sync.dma_start(dw_win[:].bitcast(I32), d_words[0].rearrange("p n t -> p (n t)").bitcast(I32))
+        for q in range(P // QUADRANT):
+            nc.sync.dma_start(
+                x_scale_win[QUADRANT * q : QUADRANT * q + 4, :].bitcast(I32),
+                x_scales[0, 4 * q : 4 * q + 4, :].bitcast(I32),
+            )
+        d_word_win = load_words("dw_win", d_words, G)
         n2_t = load_list("n2_t", n2, W)
         n1_t = load_list("n1_t", n1, W)
         n4_t = load_list("n4_t", n4, S)
-        xw_win = sb("xw_win", T, U32)
-        nc.sync.dma_start(xw_win[:].bitcast(I32), x_words[0].rearrange("p n t -> p (n t)").bitcast(I32))
+        x_word_win = load_words("xw_win", x_words, T)
         k2_t = load_list("k2_t", k2, H)
         two_t = load_list("two_t", two, S)
         cand_t = load_list("cand_t", cand, C)
@@ -88,102 +113,111 @@ def tile_picked_pqcjcrossbkmin_none_p_kernel(
         for win in a_win:
             nc.gpsimd.memset(win[:, S : S + SPARE], 0.0)
 
-        k1_raw_scales = gather("k1_raw_scales", ds_win, k1_t, H, U8)
-        k1_scales = sb("k1_scales", H, U8)
-        nc.vector.tensor_copy(
-            k1_scales[:].rearrange("p (t c i) -> p c t i", t=PACK, i=16),
-            k1_raw_scales[:].rearrange("p (c i t) -> p c t i", t=PACK, i=16),
-        )
+        k1_raw_scales = gather("k1_raw_scales", d_scale_win, k1_t, H, U8)
+        k1_scales = deal("k1_scales", k1_raw_scales, U8, LINE_BYTES)
         for r in range(1, 4):
-            nc.scalar.dma_start(k1_scales[r:P:32, :].bitcast(I32), k1_scales[8 * r : P : 32, :].bitcast(I32))
-        offs_scales = gather("offs_scales", xs_win, offs_t, S, U8)
-        k1_raw_words = gather("k1_raw_words", dw_win, k1_t, H, U32)
-        k1_words = sb("k1_words", H, U32)
-        nc.vector.tensor_copy(
-            k1_words[:].rearrange("p (t c i) -> p c t i", t=PACK, i=4),
-            k1_raw_words[:].rearrange("p (c i t) -> p c t i", t=PACK, i=4),
-        )
-        offs_words = gather("offs_words", xw_win, offs_t, S, U32)
-        banks = [psum.tile([P, 512], F32, name="bank%d" % i) for i in range(8)]
+            nc.scalar.dma_start(
+                k1_scales[r:P:QUADRANT, :].bitcast(I32), k1_scales[BLOCK_ROWS * r : P : QUADRANT, :].bitcast(I32)
+            )
+        offs_scales = gather("offs_scales", x_scale_win, offs_t, S, U8)
+        k1_raw_words = gather("k1_raw_words", d_word_win, k1_t, H, U32)
+        k1_words = deal("k1_words", k1_raw_words, U32, LINE_BYTES // 4)
+        offs_words = gather("offs_words", x_word_win, offs_t, S, U32)
+        banks = [psum.tile([P, BANK], F32, name="bank%d" % i) for i in range(2 * TILES)]
         h_win = [sb("h_win%d" % t, S, F32) for t in range(TILES)]
         for t in range(TILES):
             product(banks[t], k1_words, k1_scales, t, offs_words, offs_scales)
+        for t in range(H_ON_SCALAR, TILES):
+            nc.vector.tensor_scalar(h_win[t][:], banks[t][:, 0:S], H_SCALE, None, ALU.mult)
 
-        for t in range(2, TILES):
-            nc.vector.tensor_scalar(h_win[t][:], banks[t][:, 0:S], 0.0625, None, ALU.mult)
-        k2_raw_scales = gather("k2_raw_scales", ds_win, k2_t, H, U8)
+        k2_raw_scales = gather("k2_raw_scales", d_scale_win, k2_t, H, U8)
         for r in range(4):
-            nc.sync.dma_start(k2_scales[r:P:32, :].bitcast(I32), k2_raw_scales[8 * r : P : 32, :].bitcast(I32))
-        k2_words = gather("k2_words", dw_win, k2_t, H, U32)
-        two_words = gather("two_words", xw_win, two_t, S, U32)
-        two_scales = gather("two_scales", xs_win, two_t, S, U8)
+            nc.sync.dma_start(
+                k2_scales[r:P:QUADRANT, :].bitcast(I32), k2_raw_scales[BLOCK_ROWS * r : P : QUADRANT, :].bitcast(I32)
+            )
+        k2_words = gather("k2_words", d_word_win, k2_t, H, U32)
+        two_words = gather("two_words", x_word_win, two_t, S, U32)
+        two_scales = gather("two_scales", x_scale_win, two_t, S, U8)
         for t in range(TILES):
             product(banks[TILES + t], k2_words, k2_scales, t, two_words, two_scales)
 
         z = sb("z", S * PACK, BF16)
         z_slots = z[:].rearrange("p (j t) -> p j t", t=PACK)
-        ra = []
-        for t in range(TILES):
-            if t < 2:
-                nc.scalar.activation(h_win[t][:], banks[t][:, 0:S], COPY, scale=0.0625)
-            pa = fetch("pa%d" % t, h_win[t], n2_t, W)
-            old = fetch("old%d" % t, h_win[t], n1_t, W)
-            low = sb("low%d" % t, W, F32)
-            nc.vector.tensor_tensor(low[:], pa[:], old[:], ALU.min)
-            ra.append(sb("ra%d" % t, W, F32))
-            nc.vector.scalar_tensor_tensor(ra[t][:], pa[:], -0.5, low[:], ALU.mult, ALU.add)
-        for t in range(TILES):
-            nc.scalar.activation(h_win[t][:].indirect(n1_t[:]), ra[t][:], COPY)
+        for t in range(H_ON_SCALAR):
+            nc.scalar.activation(h_win[t][:], banks[t][:, 0:S], COPY, scale=H_SCALE)
 
-        cand_words = gather("cand_words", xw_win, cand_t, C, U32, "low2")
-        cand_scales = gather("cand_scales", xs_win, cand_t, C, U8, "low3")
+        def look_up_h(pair):
+            pa = sb("pa%d" % pair, PAIR * W, F32)
+            old = sb("old%d" % pair, PAIR * W, F32)
+            for u in range(PAIR):
+                cols = slice(W * u, W * (u + 1))
+                nc.scalar.activation(pa[:, cols], h_win[PAIR * pair + u][:].indirect(n2_t[:]), COPY)
+                nc.scalar.activation(old[:, cols], h_win[PAIR * pair + u][:].indirect(n1_t[:]), COPY)
+            return pa, old
+
+        def make_ra(pair, pa, old):
+            low = sb("low%d" % pair, PAIR * W, F32)
+            nc.vector.tensor_tensor(low[:], pa[:], old[:], ALU.min)
+            made = sb("ra%d" % pair, PAIR * W, F32)
+            nc.vector.scalar_tensor_tensor(made[:], pa[:], -0.5, low[:], ALU.mult, ALU.add)
+            return made
+
+        ra = [make_ra(0, *look_up_h(0))]
+        second_pair = look_up_h(1)
+        cand_words = gather("cand_words", x_word_win, cand_t, C, U32, "low0")
+        ra.append(make_ra(1, *second_pair))
+        for t in range(TILES):
+            u = t % PAIR
+            nc.scalar.activation(h_win[t][:].indirect(n1_t[:]), ra[t // PAIR][:, W * u : W * (u + 1)], COPY)
+        cand_scales = gather("cand_scales", x_scale_win, cand_t, C, U8, "low1")
+
         b_win = []
 
-        def empty_b(t, tag):
-            b_win.append(sb("b_win%d" % t, S + SPARE, F32, tag))
+        def empty_b(t, reuse):
+            b_win.append(sb("b_win%d" % t, S + SPARE, F32, reuse))
             nc.gpsimd.memset(b_win[t][:, S : S + SPARE], 0.0)
-            if t == 2:
-                nc.scalar.activation(b_win[t][:, 0:S], banks[TILES + t][:, 0:S], COPY, scale=0.75 * 0.0625 * 0.0625)
-            else:
-                nc.vector.tensor_scalar(b_win[t][:, 0:S], banks[TILES + t][:, 0:S], 0.75 * 0.0625 * 0.0625, None, ALU.mult)
+            nc.vector.tensor_scalar(b_win[t][:, 0:S], banks[TILES + t][:, 0:S], OUT_SCALE, None, ALU.mult)
 
-        empty_b(0, "pa3")
-        empty_b(1, "old3")
+        empty_b(0, "pa1")
+        empty_b(1, "old1")
         for t in range(TILES):
             nc.vector.tensor_scalar(z_slots[:, :, t], h_win[t][:], gs_t[:, t : t + 1], None, ALU.mult)
-
+        empty_b(2, "h_win2")
         z_words = sb("z_words", S, U32)
         z_scales = sb("z_scales", S, U8)
         nc.vector.quantize_mx(out=z_words[:].bitcast(FP8X4), scales=z_scales[:], in_=z[:])
-        empty_b(2, "ra1")
-        empty_b(3, "h_win3")
-        b4 = [fetch("b4_%d" % t, b_win[t], n4_t, S) for t in range(TILES)]
+        empty_b(3, "z")
+        b_at_n4 = []
+        for t in range(TILES):
+            b_at_n4.append(sb("b4_%d" % t, S, F32))
+            nc.scalar.activation(b_at_n4[t][:], b_win[t][:].indirect(n4_t[:]), COPY)
+
         for t in range(TILES):
             product(banks[t], cand_words, cand_scales, t, z_words, z_scales)
         for t in range(TILES):
             nc.vector.tensor_copy(a_win[t][:, 0:S], banks[t][:, 0:S])
-        OUT_SCALE = 0.75 * 0.0625 * 0.0625
+
         first = []
         for t in range(TILES):
             first.append(sb("first%d" % t, S, F32))
-            if t < 2:
-                nc.gpsimd.tensor_tensor(first[t][:], a_win[t][:, 0:S], b4[t][:], ALU.mult)
+            if t < ON_GPSIMD:
+                nc.gpsimd.tensor_tensor(first[t][:], a_win[t][:, 0:S], b_at_n4[t][:], ALU.mult)
             else:
-                nc.vector.tensor_tensor(first[t][:], banks[t][:, 0:S], b4[t][:], ALU.mult)
-        pieces = [(0, 0, S), (1, 0, S), (2, 0, S), (3, 0, S // 2), (3, S // 2, S)]
+                nc.vector.tensor_tensor(first[t][:], banks[t][:, 0:S], b_at_n4[t][:], ALU.mult)
+        pieces = [(t, 0, S) for t in range(TILES - 1)] + [(TILES - 1, 0, S // 2), (TILES - 1, S // 2, S)]
         res = [sb("res%d" % t, S, F32) for t in range(TILES)]
         second = {}
 
         def make_second(t, lo, hi):
-            a3 = sb("a3_%d_%d" % (t, lo), hi - lo, F32)
-            nc.scalar.activation(a3[:], a_win[t][:].indirect(n3_t[:, lo // 16 : hi // 16]), COPY)
+            a_at_n3 = sb("a3_%d_%d" % (t, lo), hi - lo, F32)
+            nc.scalar.activation(a_at_n3[:], a_win[t][:].indirect(n3_t[:, lo // LIST_ROWS : hi // LIST_ROWS]), COPY)
             second[t, lo] = sb("second%d_%d" % (t, lo), hi - lo, F32)
             nc.vector.scalar_tensor_tensor(
-                second[t, lo][:], banks[TILES + t][:, lo:hi], OUT_SCALE, a3[:], ALU.mult, ALU.mult
+                second[t, lo][:], banks[TILES + t][:, lo:hi], OUT_SCALE, a_at_n3[:], ALU.mult, ALU.mult
             )
 
         def finish(t, lo, hi):
-            engine = nc.gpsimd if t < 2 else nc.vector
+            engine = nc.gpsimd if t < ON_GPSIMD else nc.vector
             engine.tensor_tensor(res[t][:, lo:hi], first[t][:, lo:hi], second[t, lo][:], ALU.subtract)
             if hi == S:
                 nc.sync.dma_start(out[P * t : P * (t + 1), :], res[t][:])

from contextlib import ExitStack

import concourse.mybir as mybir

F32 = mybir.dt.float32
BF16 = mybir.dt.bfloat16
I32 = mybir.dt.int32
U32 = mybir.dt.uint32
U16 = mybir.dt.uint16
U8 = mybir.dt.uint8
FP8X4 = mybir.dt.float8_e4m3fn_x4
ALU = mybir.AluOpType
COPY = mybir.ActivationFunctionType.Copy

P = 128
K = 512
T = 1024
G = 2048
S = 256
H = 512
C = 512
W = 192
PACK = 4
TILES = 4
QUADRANT = 32
BLOCK_ROWS = 8
LIST_ROWS = 16
LINE_BYTES = 16
BANK = 512
SPARE = 8
PAIR = 2
H_ON_SCALAR = 2
ON_GPSIMD = 2
H_SCALE = 0.0625
OUT_SCALE = 0.75 * 0.0625 * 0.0625
FLOPS = 3 * 2 * K * H * S


def tile_picked_pqcjcrossbkmin_none_p_kernel(
    tc, x_words, x_scales, d_words, d_scales, gs, offs, k1, n1, n2, cand, two, k2, n3, n4, out
):
    nc = tc.nc
    with ExitStack() as ctx:
        keep = ctx.enter_context(tc.tile_pool(name="keep", bufs=1))
        psum = ctx.enter_context(tc.psum_pool(name="psum", bufs=1))

        def sb(name, width, dtype, reuse=None):
            return keep.tile([P, width], dtype, name=name, tag=reuse or name, align_bytes=64)

        def load_list(name, src, entries):
            tile = sb(name, entries // LIST_ROWS, U16)
            nc.sync.dma_start(tile[:], src)
            return tile

        def load_words(name, src, columns):
            tile = sb(name, columns, U32)
            nc.sync.dma_start(tile[:].bitcast(I32), src[0].rearrange("p n t -> p (n t)").bitcast(I32))
            return tile

        def gather(name, window, offsets, entries, dtype, reuse=None):
            tile = sb(name, entries, dtype, reuse)
            nc.vector.tensor_copy(tile[:], window[:].indirect(offsets[:]))
            return tile

        def deal(name, src, dtype, per_line):
            tile = sb(name, H, dtype)
            nc.vector.tensor_copy(
                tile[:].rearrange("p (t c i) -> p c t i", t=PACK, i=per_line),
                src[:].rearrange("p (c i t) -> p c t i", t=PACK, i=per_line),
            )
            return tile

        def product(bank, lhs_words, lhs_scales, t, rhs_words, rhs_scales):
            cols = slice(P * t, P * (t + 1))
            nc.tensor.matmul_mx(
                out=bank[:, 0:S],
                lhsT=lhs_words[:, cols].bitcast(FP8X4),
                lhsT_scale=lhs_scales[:, cols],
                rhs=rhs_words[:].bitcast(FP8X4),
                rhs_scale=rhs_scales[:],
                start=True,
                stop=True,
            )

        d_scale_win = sb("ds_win", G, U8)
        x_scale_win = sb("xs_win", T, U8)
        nc.gpsimd.memset(d_scale_win[:].bitcast(I32), 0)
        nc.gpsimd.memset(x_scale_win[:].bitcast(I32), 0)

        k1_t = load_list("k1_t", k1, H)
        nc.sync.dma_start(d_scale_win[0:P:BLOCK_ROWS, :].bitcast(I32), d_scales[0].bitcast(I32))
        offs_t = load_list("offs_t", offs, S)
        for q in range(P // QUADRANT):
            nc.sync.dma_start(
                x_scale_win[QUADRANT * q : QUADRANT * q + 4, :].bitcast(I32),
                x_scales[0, 4 * q : 4 * q + 4, :].bitcast(I32),
            )
        d_word_win = load_words("dw_win", d_words, G)
        n2_t = load_list("n2_t", n2, W)
        n1_t = load_list("n1_t", n1, W)
        n4_t = load_list("n4_t", n4, S)
        x_word_win = load_words("xw_win", x_words, T)
        k2_t = load_list("k2_t", k2, H)
        two_t = load_list("two_t", two, S)
        cand_t = load_list("cand_t", cand, C)
        n3_t = load_list("n3_t", n3, S)
        gs_t = sb("gs_t", PACK, F32)
        nc.gpsimd.dma_start(gs_t[:], gs.rearrange("(p t) o -> p (t o)", t=PACK))

        k2_scales = sb("k2_scales", H, U8)
        nc.gpsimd.memset(k2_scales[:].bitcast(I32), 0)
        a_win = [sb("a_win%d" % t, S + SPARE, F32) for t in range(TILES)]
        for win in a_win:
            nc.gpsimd.memset(win[:, S : S + SPARE], 0.0)

        k1_raw_scales = gather("k1_raw_scales", d_scale_win, k1_t, H, U8)
        k1_scales = deal("k1_scales", k1_raw_scales, U8, LINE_BYTES)
        for r in range(1, 4):
            nc.scalar.dma_start(
                k1_scales[r:P:QUADRANT, :].bitcast(I32), k1_scales[BLOCK_ROWS * r : P : QUADRANT, :].bitcast(I32)
            )
        offs_scales = gather("offs_scales", x_scale_win, offs_t, S, U8)
        k1_raw_words = gather("k1_raw_words", d_word_win, k1_t, H, U32)
        k1_words = deal("k1_words", k1_raw_words, U32, LINE_BYTES // 4)
        offs_words = gather("offs_words", x_word_win, offs_t, S, U32)
        banks = [psum.tile([P, BANK], F32, name="bank%d" % i) for i in range(2 * TILES)]
        h_win = [sb("h_win%d" % t, S, F32) for t in range(TILES)]
        for t in range(TILES):
            product(banks[t], k1_words, k1_scales, t, offs_words, offs_scales)
        for t in range(H_ON_SCALAR, TILES):
            nc.vector.tensor_scalar(h_win[t][:], banks[t][:, 0:S], H_SCALE, None, ALU.mult)

        k2_raw_scales = gather("k2_raw_scales", d_scale_win, k2_t, H, U8)
        for r in range(4):
            nc.sync.dma_start(
                k2_scales[r:P:QUADRANT, :].bitcast(I32), k2_raw_scales[BLOCK_ROWS * r : P : QUADRANT, :].bitcast(I32)
            )
        k2_words = gather("k2_words", d_word_win, k2_t, H, U32)
        two_words = gather("two_words", x_word_win, two_t, S, U32)
        two_scales = gather("two_scales", x_scale_win, two_t, S, U8)
        for t in range(TILES):
            product(banks[TILES + t], k2_words, k2_scales, t, two_words, two_scales)

        z = sb("z", S * PACK, BF16)
        z_slots = z[:].rearrange("p (j t) -> p j t", t=PACK)
        for t in range(H_ON_SCALAR):
            nc.scalar.activation(h_win[t][:], banks[t][:, 0:S], COPY, scale=H_SCALE)

        def look_up_h(pair):
            pa = sb("pa%d" % pair, PAIR * W, F32)
            old = sb("old%d" % pair, PAIR * W, F32)
            for u in range(PAIR):
                cols = slice(W * u, W * (u + 1))
                nc.scalar.activation(pa[:, cols], h_win[PAIR * pair + u][:].indirect(n2_t[:]), COPY)
                nc.scalar.activation(old[:, cols], h_win[PAIR * pair + u][:].indirect(n1_t[:]), COPY)
            return pa, old

        def make_ra(pair, pa, old):
            low = sb("low%d" % pair, PAIR * W, F32)
            nc.vector.tensor_tensor(low[:], pa[:], old[:], ALU.min)
            made = sb("ra%d" % pair, PAIR * W, F32)
            nc.vector.scalar_tensor_tensor(made[:], pa[:], -0.5, low[:], ALU.mult, ALU.add)
            return made

        ra = [make_ra(0, *look_up_h(0))]
        second_pair = look_up_h(1)
        cand_words = gather("cand_words", x_word_win, cand_t, C, U32, "low0")
        ra.append(make_ra(1, *second_pair))
        for t in range(TILES):
            u = t % PAIR
            nc.scalar.activation(h_win[t][:].indirect(n1_t[:]), ra[t // PAIR][:, W * u : W * (u + 1)], COPY)
        cand_scales = gather("cand_scales", x_scale_win, cand_t, C, U8, "low1")

        b_win = []

        def empty_b(t, reuse):
            b_win.append(sb("b_win%d" % t, S + SPARE, F32, reuse))
            nc.gpsimd.memset(b_win[t][:, S : S + SPARE], 0.0)
            nc.vector.tensor_scalar(b_win[t][:, 0:S], banks[TILES + t][:, 0:S], OUT_SCALE, None, ALU.mult)

        empty_b(0, "pa1")
        empty_b(1, "old1")
        for t in range(TILES):
            nc.vector.tensor_scalar(z_slots[:, :, t], h_win[t][:], gs_t[:, t : t + 1], None, ALU.mult)
        empty_b(2, "h_win2")
        z_words = sb("z_words", S, U32)
        z_scales = sb("z_scales", S, U8)
        nc.vector.quantize_mx(out=z_words[:].bitcast(FP8X4), scales=z_scales[:], in_=z[:])
        empty_b(3, "z")
        b_at_n4 = []
        for t in range(TILES):
            b_at_n4.append(sb("b4_%d" % t, S, F32))
            nc.scalar.activation(b_at_n4[t][:], b_win[t][:].indirect(n4_t[:]), COPY)

        for t in range(TILES):
            product(banks[t], cand_words, cand_scales, t, z_words, z_scales)
        for t in range(TILES):
            nc.vector.tensor_copy(a_win[t][:, 0:S], banks[t][:, 0:S])

        first = []
        for t in range(TILES):
            first.append(sb("first%d" % t, S, F32))
            if t < ON_GPSIMD:
                nc.gpsimd.tensor_tensor(first[t][:], a_win[t][:, 0:S], b_at_n4[t][:], ALU.mult)
            else:
                nc.vector.tensor_tensor(first[t][:], banks[t][:, 0:S], b_at_n4[t][:], ALU.mult)
        pieces = [(t, 0, S) for t in range(TILES - 1)] + [(TILES - 1, 0, S // 2), (TILES - 1, S // 2, S)]
        res = [sb("res%d" % t, S, F32) for t in range(TILES)]
        second = {}

        def make_second(t, lo, hi):
            a_at_n3 = sb("a3_%d_%d" % (t, lo), hi - lo, F32)
            nc.scalar.activation(a_at_n3[:], a_win[t][:].indirect(n3_t[:, lo // LIST_ROWS : hi // LIST_ROWS]), COPY)
            second[t, lo] = sb("second%d_%d" % (t, lo), hi - lo, F32)
            nc.vector.scalar_tensor_tensor(
                second[t, lo][:], banks[TILES + t][:, lo:hi], OUT_SCALE, a_at_n3[:], ALU.mult, ALU.mult
            )

        def finish(t, lo, hi):
            engine = nc.gpsimd if t < ON_GPSIMD else nc.vector
            engine.tensor_tensor(res[t][:, lo:hi], first[t][:, lo:hi], second[t, lo][:], ALU.subtract)
            if hi == S:
                nc.sync.dma_start(out[P * t : P * (t + 1), :], res[t][:])

        make_second(*pieces[0])
        for before, piece in zip(pieces, pieces[1:]):
            make_second(*piece)
            finish(*before)
        finish(*pieces[-1])
